import numpy as np, ml_dtypes
CORES = [16,17,18,19,32,33,34,35]
N = 8
BF = ml_dtypes.bfloat16
def gentries(a):
    return np.ascontiguousarray(a.reshape(8, 16, -1).transpose(0, 2, 1)).reshape(8, -1)
def gtable(e):
    e = np.asarray(e); return np.ascontiguousarray(e.reshape(8, -1, 16).transpose(0, 2, 1)).reshape(128, -1).astype(np.int32)
NO, D, B, K, RO, TH = 20, 4, 160, 8, 5, 9
V, NB = NO * B, NO + D
def every(z):
    return np.concatenate([z, np.stack([np.roll(z[:, :, d - 1], d, axis=0) for d in range(1, D + 1)], axis=2)], axis=2)
def parts(rng):
    a = rng.integers(0, 256, (N, 8, 15, V)); m = (rng.random((N, 8, V)) < 0.0625).astype(np.int64)
    u = np.argsort(rng.random((N, 8, NB, V)), axis=-1)[..., :16 * B].reshape(N, 8, NB, 16, B)
    e = np.argsort(rng.random((N, 8, NO, B)), axis=-1)[..., :K]
    return a, m, u, np.ascontiguousarray(e)
def firsts(e):
    z = np.zeros((N, 8, V), bool); np.put_along_axis(z, (e + B * np.arange(NO)[:, None]).reshape(N, 8, -1), True, 2)
    return z
def reach(u, e):
    z = np.zeros((N, 8, V), bool); q = np.take_along_axis(u, every(e)[:, :, :, None, :], 4)
    np.put_along_axis(z, q.reshape(N, 8, -1), True, 2)
    return z
def cover(rng):
    o = np.argsort(rng.random((N, V)), axis=-1)
    return np.stack([np.roll(o, -16 * K * c, axis=1) for c in range(NB)], axis=1)
def aim(rng, e, g, o):
    ee = every(e)[:, g]; w = np.zeros((N, NB, 16, B), np.int64)
    for r in range(N):
        for c in range(NB):
            rest = np.ones(B, bool); rest[ee[r, c]] = False
            w[r, c][:, ee[r, c]] = o[r, c, :16 * K].reshape(16, K)
            w[r, c][:, rest] = rng.permutation(o[r, c, 16 * K:])[:16 * (B - K)].reshape(16, B - K)
    return w
def pack(a, m, u, e):
    rec = np.concatenate([a, m[:, :, None]], axis=2).reshape(N, 128, V).astype(np.float32).astype(BF)
    up = np.ascontiguousarray(u.transpose(0, 1, 3, 2, 4).reshape(N, 128, NB * B)).astype(np.int32)
    return {"rec": rec, "up": up, "fr": np.stack([gtable(z.reshape(8, -1)) for z in e])}
def setup_inputs(rng):
    return pack(*parts(rng))
def setup_inputs_room(rng):
    a, m, u, e = parts(rng); c = reach(u, e); z = firsts(e); can = c & ~z; pick = np.zeros((N, 8, V), bool)
    for r in range(N):
        for g in range(8):
            for b in range(NO):
                o = b * B + rng.permutation(np.flatnonzero(can[r, g, b * B:(b + 1) * B])); n = int(rng.choice(np.array([0, 1, K - 1, K, K + 1, B])))
                if r == 0 and b == 0: n = (K, K + 1, B, K - 1, 1, 0, K, K + 1)[g]
                pick[r, g, o[:n]] = True
    a = np.where(c[:, :, None], np.where(pick[:, :, None], rng.integers(150, 256, a.shape), rng.integers(0, 51, a.shape)), a)
    a = np.where(z[:, :, None], rng.integers(100, 111, a.shape), a)
    return pack(a, z.astype(np.int64), u, e)
def setup_inputs_ties(rng):
    a, m, u, e = parts(rng); z = firsts(e)
    lo = np.array([0, 254, 100, 0, 7, 127, 1, 128]).reshape(1, 8, 1, 1); step = np.array([1, 1, 1, 255, 1, 1, 2, 1]).reshape(1, 8, 1, 1)
    p = np.where(z, 0.6, 0.15 + 0.3 * rng.random((N, 8, V)))[:, :, None]
    a = lo + step * (rng.random(a.shape) < p)
    a[:, 1] = np.where((rng.random((N, V)) < 0.6)[:, None], 255, a[:, 1])
    return pack(a, m, u, e)
def setup_inputs_meet(rng):
    a, m, u, e = parts(rng)
    u[:, ::2] = u[:, ::2, :1].copy(); e[:, ::2] = e[:1, ::2, :1].copy()
    i = 1 + np.argsort(rng.random((N, 4, NO, B - 2)), axis=-1)[..., :K - 2]
    e[:, 1::2, :, 2:] = i; e[:, 1::2, :, 0] = 0; e[:, 1::2, :, 1] = B - 1
    base = np.arange(16 * B).reshape(B, 16).T; u[:, 1] = base; u[:, 1, NO:] = base + V - 16 * B
    o = np.argsort((np.arange(V) + rng.integers(0, 16, (N, 1, 1))) % 16 + rng.random((N, 1, V)), axis=-1)
    u[:, 2] = aim(rng, e, 2, np.broadcast_to(o, (N, NB, V)))[:, :1]
    u[:, 3] = aim(rng, e, 3, cover(rng)); z = firsts(e)
    a[:, 3] = np.where(z[:, 3][:, None], rng.integers(0, 51, (N, 15, V)), rng.integers(150, 256, (N, 15, V))); m[:, 3] = 0
    return pack(a, m, u, e)
def setup_inputs_dry(rng):
    a, m, u, e = parts(rng); z = firsts(e); o = rng.permutation(8)
    a[:, o[1]] = np.where(z[:, o[1]][:, None], rng.integers(100, 256, (N, 15, V)), rng.integers(0, 100, (N, 15, V)))
    for g in (o[3], o[4]):
        a[:, g] = np.where(rng.random((N, 15, V)) < 0.7, 255, rng.integers(0, 101, (N, 15, V)))
    a[:, o[3], :, ::B] = 0
    u[:, o[5]] = aim(rng, e, o[5], cover(rng))
    a[:, o[5]] = np.where(z[:, o[5]][:, None], rng.integers(0, 31, (N, 15, V)), rng.integers(80, 256, (N, 15, V)))
    a[:, o[5], :, ::B] = rng.integers(60, 101, (N, 15, NO))
    m[:, o[0]] = 1; m[:, o[2]] = rng.random((N, V)) < 0.9; m[:, o[3]] = 1; m[:, o[4]] = rng.random((N, V)) < 0.95
    m[:, o[5]] = 1; m[:, o[5], ::B] = 0
    m[(rng.integers(-2, 1) + np.arange(3)) % N] = 1
    return pack(a, m, u, e)
def setup_inputs_spread(rng):
    a, m, u, e = parts(rng); s = np.exp2(8.2 * rng.random((N, 8, 1, V)))
    a = np.minimum((s * rng.random(a.shape)).astype(np.int64), 255); m = (rng.random(m.shape) < rng.random((N, 8, 1)) * 0.5).astype(np.int64)
    return pack(a, m, u, e)
def check_inputs(d):
    bad = []
    r = d["rec"].astype(np.float32).reshape(N, 8, 16, V); a, m = r[:, :, :15], r[:, :, 15]
    if not np.all((a >= 0) & (a <= 255) & (a == np.floor(a))): bad.append("notes in rec")
    if not np.all((m == 0) | (m == 1)): bad.append("marks in rec")
    if np.min(d["up"]) < 0 or np.max(d["up"]) > V - 1: bad.append("range of up")
    u = np.sort(d["up"].reshape(N, 8, 16, NB, B).transpose(0, 1, 3, 2, 4).reshape(N, 8, NB, 16 * B), axis=-1)
    if np.any(u[..., 1:] == u[..., :-1]): bad.append("different parents in a bank of up")
    if np.min(d["fr"]) < 0 or np.max(d["fr"]) > B - 1: bad.append("range of fr")
    e = np.sort(np.stack([gentries(z) for z in d["fr"]]).reshape(N, 8, NO, K), axis=-1)
    if np.any(e[..., 1:] == e[..., :-1]): bad.append("different places in a bank of fr")
    return bad
def reference(rec, up, fr):
    s = rec.astype(np.float32).astype(np.int64).reshape(N, 8, 16, V); a = s[:, :, :15].copy(); mark = s[:, :, 15] > 0
    u = up.astype(np.int64).reshape(N, 8, 16, NB, B)
    e = np.stack([gentries(z) for z in fr]).astype(np.int64).reshape(N, 8, NO, K); live = np.ones(e.shape, bool)
    for wave in range(RO):
        node = e + B * np.arange(NO)[:, None]
        x = np.take_along_axis(a, node.reshape(N, 8, 1, NO * K), 3).reshape(N, 8, 15, NO, K)
        ee, ll, xx = every(e), every(live), every(np.moveaxis(x, 2, 3))
        new = a.copy(); hit = np.zeros((N, 8, V), bool)
        for b in range(NB):
            q = np.take_along_axis(u[:, :, :, b], ee[:, :, None, b], 3).reshape(N, 8, 1, 16 * K)
            old = np.take_along_axis(a, q, 3)
            arr = np.tile(xx[:, :, b], (1, 1, 1, 16))
            ok = (np.add.reduce((old >= arr).astype(np.int64), axis=2) >= TH) & np.tile(ll[:, :, b], (1, 1, 16))
            r, g, j = np.nonzero(ok); to = q[r, g, 0, j]
            new[r, g, :, to] = ((old + arr) >> 1)[r, g, :, j]
            hit[r, g, to] = True
        h = (hit & ~mark).reshape(N, 8, NO, B); mark = mark | hit; a = new
        e = np.argsort(~h, axis=-1, kind="stable")[..., :K]; live = np.take_along_axis(h, e, 3)
    return {"y": np.concatenate([a, mark[:, :, None].astype(np.int64)], axis=2).reshape(N, 128, V).astype(np.float32).astype(BF)}

import numpy as np
from concourse.bass import DstId, RemoteDMATransfer
from concourse.mybir import AluOpType as OP, ActivationFunctionType as AF

V, NO, B, K, RO, D = 3200, 20, 160, 8, 5, 4
SENT = V
GH = V + 16
UPW = GH + D * B + 16
STEP, SHIFT = 1680, 4896
WIN = SHIFT + 15 * STEP + 128
MAGIC = 8388608.0
PKW = 34
SLOT = 48

SCRATCH = {
    "St0": ("sbuf", [128, WIN], "bfloat16"), "St1": ("sbuf", [128, WIN], "bfloat16"),
    "UPS": ("sbuf", [128, UPW], "int32"), "FR": ("sbuf", [128, 10], "int32"),
    "OG": ("sbuf", [128, 3072], "bfloat16"), "CM": ("sbuf", [128, 3072], "bfloat16"), "OF": ("sbuf", [128, 3072], "bfloat16"),
    "LF": ("sbuf", [128, 48], "float32"), "LP": ("sbuf", [128, 12], "uint16"),
    "PQ": ("sbuf", [128, 192], "uint16"), "QF": ("sbuf", [128, 192], "float32"),
    "XF": ("sbuf", [128, 192], "float32"), "OX": ("sbuf", [128, 192], "uint16"),
    "PK": ("sbuf", [128, RO * SLOT], "bfloat16"), "LAND": ("sbuf", [128, RO * D * SLOT], "bfloat16"),
    "XG": ("sbuf", [128, 128], "bfloat16"), "GX": ("sbuf", [128, 32], "bfloat16"),
    "XT0": ("sbuf", [128, 128], "bfloat16"), "XT1": ("sbuf", [128, 128], "bfloat16"),
    "XT2": ("sbuf", [128, 128], "bfloat16"), "XT3": ("sbuf", [128, 128], "bfloat16"),
    "MB": ("sbuf", [128, 1600], "bfloat16"), "CC": ("sbuf", [128, 1600], "bfloat16"),
    "IN": ("sbuf", [128, 1600], "bfloat16"), "PC": ("sbuf", [128, 1600], "bfloat16"), "RST": ("sbuf", [128, 1600], "bfloat16"),
    "ONE": ("sbuf", [128, 1536], "bfloat16"), "E0": ("sbuf", [128, 1536], "bfloat16"),
    "ED": ("sbuf", [128, 1536], "bfloat16"), "ES": ("sbuf", [128, 1536], "bfloat16"),
    "ID": ("sbuf", [128, 128], "bfloat16"), "IZ": ("sbuf", [128, 128], "bfloat16"), "HB": ("sbuf", [128, 128], "bfloat16"),
    "Z": ("sbuf", [128, 144], "bfloat16"), "T8": ("sbuf", [128, 16], "bfloat16"), "TR": ("sbuf", [128, 32], "bfloat16"),
    "TI": ("sbuf", [128, 32], "float32"),
    "S0": ("sbuf", [128, 128], "bfloat16"), "S1": ("sbuf", [128, 128], "bfloat16"), "MAG": ("sbuf", [128, 128], "bfloat16"),
    "KI": ("sbuf", [128, 8], "int32"), "CF": ("sbuf", [128, 64], "float32"), "CB": ("sbuf", [128, 2], "bfloat16"),
}
for _i in range(8):
    SCRATCH["P%d" % _i] = ("psum", [128, 512], "float32")
SEMAPHORES = ["sP", "sA", "sD", "sG", "dfr", "drec", "dup0", "dup1", "dup2", "dup3", "dup4", "dup5", "dy", "snt"] + ["arr%d" % w for w in range(RO)]


def rank_program(g, core, T, topo):
    rank = T.rank_of(core)
    if rank is None:
        return
    queues = {"P": g.tensor, "A": g.scalar, "D": g.vector, "G": g, "S": g.sync}
    count = {"P": 0, "A": 0, "D": 0, "G": 0}
    know = {q: {} for q in queues}
    hist = {}

    def deps(q, reads, writes):
        found = []
        for acc, wr in ((reads, False), (writes, True)):
            for buf, a, b in acc:
                psum = buf[0] == "P" and buf[1:].isdigit()
                for e in hist.get(buf, []):
                    if psum:
                        if e[3] != q:
                            found.append(e)
                    elif e[0] < b and e[1] > a:
                        if e[2] or (wr and e[3] != q):
                            found.append(e)
        k = know[q]
        best = {}
        for e in found:
            if k.get(e[4], 0) >= e[5] or any(f is not e and f[6].get(e[4], 0) >= e[5] for f in found):
                continue
            best[e[4]] = max(best.get(e[4], 0), e[5])
        for s, v in best.items():
            queues[q].wait_ge(T.sem[s], v)
        for e in found:
            k[e[4]] = max(k.get(e[4], 0), e[5])
            for s, v in e[6].items():
                k[s] = max(k.get(s, 0), v)

    def note(q, reads, writes, sem, val, snap):
        for acc, wr in ((reads, False), (writes, True)):
            for buf, a, b in acc:
                h = hist.setdefault(buf, [])
                if wr:
                    h[:] = [e for e in h if not (a <= e[0] and e[1] <= b)]
                else:
                    h[:] = [e for e in h if not (not e[2] and e[3] == q and e[4] == sem and a <= e[0] and e[1] <= b)]
                h.append((a, b, wr, q, sem, val, snap))

    def run(q, reads, writes, f):
        deps(q, reads, writes)
        snap = dict(know[q])
        count[q] += 1
        f().then_inc(T.sem["s" + q], 1)
        note(q, reads, writes, "s" + q, count[q], snap)

    def dma(q, sem, reads, writes, out, in_):
        deps(q, reads, writes)
        snap = dict(know[q])
        queues[q].dma_start(out, in_).then_inc(T.sem[sem], 16)
        note("dma" + sem, reads, writes, sem, 16, snap)

    vec, act, ten = g.vector, g.scalar, g.tensor

    def ap(x, n=128, p0=0):
        s = x[3] if len(x) > 3 else 1
        return T[x[0]][p0:p0 + n, x[1]:x[2]:s] if s != 1 else T[x[0]][p0:p0 + n, x[1]:x[2]]

    def rg(*xs):
        return [x[:3] for x in xs]

    def memset(x, c, n=128, p0=0):
        run("D", [], rg(x), lambda: vec.memset(ap(x, n, p0), c))

    def ts(out, in0, s1, s2, op0, op1=None, n=128):
        rd = [in0] + [s for s in (s1, s2) if isinstance(s, tuple)]
        a1 = ap(s1, n) if isinstance(s1, tuple) else s1
        a2 = ap(s2, n) if isinstance(s2, tuple) else s2
        if op1 is None:
            run("D", rg(*rd), rg(out), lambda: vec.tensor_scalar(ap(out, n), ap(in0, n), a1, None, op0))
        else:
            run("D", rg(*rd), rg(out), lambda: vec.tensor_scalar(ap(out, n), ap(in0, n), a1, a2, op0, op1))

    def tt(out, a, b, op):
        run("D", rg(a, b), rg(out), lambda: vec.tensor_tensor(ap(out), ap(a), ap(b), op))

    def cp(out, in_):
        run("D", rg(in_), rg(out), lambda: vec.tensor_copy(ap(out), ap(in_)))

    def acp(out, in_, n=128):
        run("A", rg(in_), rg(out), lambda: act.activation(ap(out, n), ap(in_, n), AF.Copy))

    def mm(out, lhsT, rhs, start, stop, m=128, k=128):
        run("P", rg(lhsT, rhs), rg(out), lambda: ten.matmul(ap(out, m), ap(lhsT, k), ap(rhs, k), start, stop))

    dma("S", "dfr", [], [("FR", 0, 10)], T.FR[:], T.fr[:])
    dma("A", "dup0", [], [("UPS", 0, 640)], T.UPS[:, 0:640], T.up[:, 0:640])
    dma("S", "drec", [], [("St0", 0, V)], T.St0[:, 0:V], T.rec[:])
    for i in range(1, 5):
        dma("SA"[i % 2], "dup%d" % i, [], [("UPS", 640 * i, 640 * i + 640)], T.UPS[:, 640 * i:640 * i + 640], T.up[:, 640 * i:640 * i + 640])
    dma("S", "dup5", [], [("UPS", GH, GH + 640)], T.UPS[:, GH:GH + 640], T.up[:, V:V + 640])

    memset(("ONE", 0, 1536), 1.0)

    def iota(x, pat, base, cm, small=True):
        if small:
            run("G", [], rg(x), lambda: g.iota(ap(x), pat, base, cm, allow_small_or_imprecise_dtypes=True))
        else:
            run("G", [], rg(x), lambda: g.iota(ap(x), pat, base, cm))

    def sel(out, in_, pat, op, base, cm, n=128):
        run("G", rg(in_), rg(out), lambda: g.affine_select(ap(out, n), ap(in_, n), pat, op, 0.0, base, cm))

    iota(("KI", 0, 1), [[0, 1]], 0, 1, False)
    iota(("CF", 16, 26), [[320, 10]], 0, 0)
    iota(("CF", 32, 34), [[320, 2]], GH, 0)
    iota(("TI", 0, 32), [[0, 4], [16, 8]], 0, 0)
    sel(("ID", 0, 128), ("ONE", 0, 128), [[-1, 128]], OP.is_equal, 0, 1)
    sel(("E0", 0, 1536), ("ONE", 0, 1536), [[-1, 96], [0, 16]], OP.is_equal, 0, 1, n=96)
    sel(("T8", 0, 8), ("ONE", 0, 8), [[-16, 8]], OP.is_ge, 0, 1)
    sel(("T8", 8, 16), ("T8", 0, 8), [[16, 8]], OP.is_ge, 14, -1)
    sel(("S0", 0, 128), ("ONE", 0, 128), [[-16, 8], [-1000, 2], [0, 8]], OP.is_equal, -15, 1)
    sel(("S1", 0, 128), ("ONE", 0, 128), [[-16, 8], [-1000, 2], [0, 8]], OP.is_equal, 985, 1)

    C = {n: ("CF", j, j + 1) for j, n in enumerate(["p", "m0", "p160", "r", "scol", "hbias", "lscale", "lbias", "hcol", "t"])}
    THR, CAP = ("CB", 0, 1), ("CB", 1, 2)
    ts(("KI", 1, 2), ("KI", 0, 1), 3, 1, OP.logical_shift_right, OP.bitwise_and)
    ts(("KI", 2, 3), ("KI", 0, 1), 7, None, OP.bitwise_and)
    ts(("KI", 3, 4), ("KI", 0, 1), 15, None, OP.bitwise_and)
    cp(C["p"], ("KI", 1, 2))
    ts(C["p160"], ("KI", 1, 2), 160.0, None, OP.mult)
    ts(("CF", 36, 46), ("CF", 16, 26), C["p160"], None, OP.add)
    ts(("CF", 46, 48), ("CF", 32, 34), C["p160"], None, OP.add)
    cp(("LF", 0, 10), ("FR", 0, 10))
    cp(C["t"], ("KI", 3, 4))
    ts(C["r"], C["t"], 15.0, None, OP.is_equal)
    ts(C["scol"], C["r"], -2.0, 1.0, OP.mult, OP.add)
    ts(CAP, C["r"], -254.0, 255.0, OP.mult, OP.add)
    ts(C["m0"], C["p"], -1.0, 1.0, OP.mult, OP.add)
    ts(C["hbias"], C["r"], -MAGIC, None, OP.add)
    ts(C["lscale"], C["r"], -1.0, 1.0, OP.mult, OP.add)
    ts(C["lbias"], C["r"], MAGIC + 1.0, -MAGIC, OP.mult, OP.add)
    ts(C["hcol"], C["r"], 254.5, 0.5, OP.mult, OP.add)
    ts(THR, ("KI", 2, 3), 256.0, 256.0, OP.mult, OP.add)
    for x in ("XT0", "XT1", "XT2", "XT3"):
        memset((x, 0, 128), 0.0)
        memset((x, 0, 128), -0.25, n=1, p0=96)
    memset(("MAG", 0, 128), MAGIC)
    memset(("Z", 0, 144), 0.0)
    memset(("St0", V, V + 16), 512.0)
    memset(("St1", V, V + 16), 512.0)
    memset(("UPS", V, V + 16), 0)
    memset(("UPS", GH + 640, UPW), 0)
    ts(("IZ", 0, 128), ("ID", 0, 128), C["lscale"], None, OP.mult)
    ts(("HB", 0, 128), ("ID", 0, 128), C["hcol"], None, OP.mult)

    def late_constants():
        ts(("ED", 0, 1536), ("E0", 0, 1536), -1.0, None, OP.mult, n=96)
        memset(("ES", 0, 1536), 1.0, n=1, p0=96)
        ts(("ES", 0, 1536), ("E0", 0, 1536), 0.5, None, OP.mult, n=96)
        ts(("Z", 15, 128, 16), ("T8", 8, 16), float(-STEP), None, OP.mult)
        ts(("TR", 0, 32), ("TI", 0, 32), C["t"], None, OP.add)
        memset(("RST", 0, 1600), 1.0)
        memset(("RST", 0, 1600, 160), 0.0)

    dests = [T.cores[(rank + d) % 8] for d in range(1, D + 1)]
    pick, used = {}, set()
    for dst in sorted(dests, key=lambda c: len(topo.engines(core, c))):
        e = [x for x in topo.engines(core, dst) if x not in used][:2]
        used.update(e)
        pick[dst] = sum(1 << x for x in e)

    for w in range(RO):
        X, Y = "St%d" % (w % 2), "St%d" % ((w + 1) % 2)
        last = w == RO - 1
        pk = SLOT * w

        def gather_up(c0, c1, win):
            a, b = 16 * c0, 16 * c1
            run("D", [("LP", c0, c1), ("UPS", 0, win)], [("PQ", a, b)],
                lambda: vec.tensor_copy(T.PQ[:, a:b], T.UPS[:, 0:win].indirect(T.LP[:, c0:c1])))
            ts(("QF", a, b), ("PQ", a, b), float(-SHIFT), None, OP.add)

        def gather_x(out, c0, c1):
            run("A", [("LP", c0, c1), (X, 0, GH)], rg(out),
                lambda: act.activation(ap(out), T[X][:, 0:GH].indirect(T.LP[:, c0:c1]), AF.Copy))

        def gather_old(i):
            run("A", [("PQ", 32 * i, 32 * i + 32), (X, 0, GH), C["scol"], C["r"]], [("OG", 512 * i, 512 * i + 512)],
                lambda: act.activation(T.OG[:, 512 * i:512 * i + 512], T[X][:, 0:GH].indirect(T.PQ[:, 32 * i:32 * i + 32]), AF.Relu,
                                       bias=ap(C["r"]), scale=ap(C["scol"])))

        def xtile(i):
            return ("XT0", "XT1", "XT1", "XT1", "XT2", "XT3")[i], 512 * (0, 0, 1, 2, 0, 0)[i]

        def diff(i):
            d, (x, e) = "P%d" % (3 + i % 2), xtile(i)
            mm((d, 0, 512), ("ID", 0, 128), ("OG", 512 * i, 512 * i + 512), True, False)
            mm((d, 0, 512), (x, 0, 128), ("ED", e, e + 512), False, True, k=96)

        def half(i):
            s, (x, e) = "P%d" % (5 + i % 2), xtile(i)
            mm((s, 0, 512), (x, 0, 128), ("ES", e, e + 512), True, False, k=97)
            mm((s, 0, 512), ("HB", 0, 128), ("OG", 512 * i, 512 * i + 512), False, False)
            mm((s, 0, 512), ("MAG", 0, 128), ("ONE", 0, 512), False, True, k=1)

        def signs(i):
            d = "P%d" % (3 + i % 2)
            run("A", [(d, 0, 512)], [("CM", 512 * i, 512 * i + 512)],
                lambda: act.activation(T.CM[:, 512 * i:512 * i + 512], T[d][:, 0:512], AF.Sign, bias=0.5))

        def offers(i):
            s = "P%d" % (5 + i % 2)
            bias, scale = (C["lbias"], C["lscale"]) if last else (C["hbias"], None)
            if scale is None:
                run("A", [(s, 0, 512), bias], [("OF", 512 * i, 512 * i + 512)],
                    lambda: act.activation(T.OF[:, 512 * i:512 * i + 512], T[s][:, 0:512], AF.Identity, bias=ap(bias)))
            else:
                run("A", [(s, 0, 512), bias, scale], [("OF", 512 * i, 512 * i + 512)],
                    lambda: act.activation(T.OF[:, 512 * i:512 * i + 512], T[s][:, 0:512], AF.Identity, bias=ap(bias), scale=ap(scale)))

        def counts(i):
            c = "P%d" % (1 + i % 2)
            mm((c, 0, 32), ("ID", 0, 128), ("TR", 0, 32), True, False)
            for t in range(16):
                mm((c, 0, 32), ("Z", 15 - t, 143 - t), ("CM", 512 * i + t, 512 * i + 512, 16), False, t == 15)

        def scatter(i):
            a, b = 32 * i, 32 * i + 32
            tt(("XF", a, b), ("P%d" % (1 + i % 2), 0, 32), ("QF", a, b), OP.max)
            ts(("OX", a, b), ("XF", a, b), float(SHIFT), None, OP.add)
            for c in range(4 * i, 4 * i + 4):
                run("D", [("OX", 8 * c, 8 * c + 8), ("OF", 128 * c, 128 * c + 128)], [(Y, 0, WIN)],
                    lambda: vec.tensor_copy(T[Y][:, 0:WIN].indirect(T.OX[:, 8 * c:8 * c + 8]), T.OF[:, 128 * c:128 * c + 128]))

        def marks(bank, pairs):
            for n, c in enumerate(pairs):
                for p in (0, 1):
                    b = 2 * c + p
                    mm((bank, 160 * n, 160 * n + 160), ("S%d" % p, 0, 128), (X, 160 * b, 160 * b + 160), p == 0, p == 1)

        def places(a, b):
            run("D", [("RST", a, b), ("MB", a, b)], [("CC", a, b)],
                lambda: vec.tensor_tensor_scan(T.CC[:, a:b], T.RST[:, a:b], T.MB[:, a:b], 0.0, OP.mult, OP.add))
            ts(("IN", a, b), ("CC", a, b), THR, None, OP.is_lt)
            run("D", [("RST", a, b), ("IN", a, b)], [("PC", a, b)],
                lambda: vec.tensor_tensor_scan(T.PC[:, a:b], T.RST[:, a:b], T.IN[:, a:b], 0.0, OP.mult, OP.add))

        def fresh_copy():
            ts((Y, 0, V), (X, 0, V), CAP, None, OP.min)

        def xt(bank, col, src, n):
            mm((bank, col, col + 128), src, ("IZ", 0, 128), True, True, m=n)

        def xtcopy(out, bank, col, n):
            acp((out, 0, 128), (bank, col, col + 128), n=n)

        def send():
            deps("G", [("PK", pk, pk + PKW)], [])
            g.remote_dma_fused([RemoteDMATransfer(
                dst_ids=[DstId(rid=topo.addr(dst)[0], pnc=topo.addr(dst)[1])], dma_engine_mask=pick[dst], remote_sem=T.sem["arr%d" % w],
                src=T.PK[:, pk:pk + PKW], dst=T.LAND[:, SLOT * (D * w + d):SLOT * (D * w + d) + PKW]) for d, dst in enumerate(dests)],
                local_sem=T.sem.snt)
            note("R", [], [("LAND", SLOT * D * w, SLOT * D * (w + 1))], "arr%d" % w, 2 * D, {})
            for d in range(D):
                s = SLOT * (D * w + d) + 8 * d
                sel(("GX", 8 * d, 8 * d + 8), ("LAND", s, s + 8), [[0, 8]], OP.is_ge, 1, 0)

        def ghosts():
            for c in range(2):
                s1, s2 = SLOT * (D * w + 2 * c) + 32 + c, SLOT * (D * w + 2 * c + 1) + 32 + c
                ts(("LF", 24 + c, 25 + c), ("LAND", s1, s1 + 1), C["m0"], ("CF", 46 + c, 47 + c), OP.mult, OP.add)
                ts(("LP", 10 + c, 11 + c), ("LAND", s2, s2 + 1), C["p"], ("LF", 24 + c, 25 + c), OP.mult, OP.add)
            gather_up(10, 12, UPW)

        if w == 0:
            tt(("LF", 12, 22), ("LF", 0, 10), ("CF", 36, 46), OP.add)
            cp(("LP", 0, 10), ("LF", 12, 22))
            acp(("PK", pk + 32, pk + 34), ("LF", 0, 2))
            gather_up(0, 2, 640)
            late_constants()
        else:
            marks("P0", range(0, 2))
            acp(("MB", 0, 320), ("P0", 0, 320))
            for bank, c0, c1 in (("P4", 2, 5), ("P6", 5, 8), ("P7", 8, 10)):
                marks(bank, range(c0, c1))
                acp(("MB", 160 * c0, 160 * c1), (bank, 0, 160 * (c1 - c0)))
            places(0, 320)
            acp(("PK", pk + 32, pk + 34), ("PC", 159, 320, 160))
            ts(("LF", 0, 2), ("PC", 159, 320, 160), 160.0, float(SENT), OP.is_ge, OP.mult)
            for c in range(2):
                ts(("LP", c, c + 1), ("PC", 160 * c + 159, 160 * c + 160), ("CF", 36 + c, 37 + c), ("LF", c, c + 1), OP.add, OP.max)
            gather_up(0, 2, UPW)

        gather_x(("PK", pk, pk + 32), 0, 2)
        gather_old(0)
        xt("P0", 0, ("PK", pk, pk + 32), 32)
        xtcopy("XT0", "P0", 0, 32)
        send()
        diff(0)
        half(0)
        signs(0)
        counts(0)
        offers(0)

        if w > 0:
            places(320, 1600)
            tt(("LF", 12, 20), ("PC", 479, 1600, 160), ("CF", 38, 46), OP.add)
            ts(("LF", 2, 10), ("PC", 479, 1600, 160), 160.0, float(SENT), OP.is_ge, OP.mult)
            tt(("LF", 26, 34), ("LF", 12, 20), ("LF", 2, 10), OP.max)
            cp(("LP", 2, 10), ("LF", 26, 34))
            gather_up(2, 10, UPW)
            fresh_copy()
        else:
            fresh_copy()
            gather_up(2, 4, 1280)
        gather_x(("XG", 0, 128), 2, 10)
        xt("P7", 0, ("XG", 0, 96), 96)
        xt("P7", 128, ("XG", 96, 128), 32)
        xtcopy("XT1", "P7", 0, 96)
        xtcopy("XT2", "P7", 128, 32)
        scatter(0)
        gather_old(1)
        diff(1)
        half(1)
        for i in range(1, 6):
            if i < 5:
                if w == 0 and i < 4:
                    gather_up(2 * i + 2, 2 * i + 4, 640 * i + 1280)
                if i == 4:
                    xt("P7", 256, ("GX", 0, 32), 32)
                    xtcopy("XT3", "P7", 256, 32)
                gather_old(i + 1)
                diff(i + 1)
            signs(i)
            counts(i)
            offers(i)
            if i < 5:
                half(i + 1)
            scatter(i)
            if i == 2:
                ghosts()

    dma("S", "dy", [("St%d" % (RO % 2), 0, V)], [], T.y[:], T["St%d" % (RO % 2)][:, 0:V])
    for q in "PADG":
        g.wait_ge(T.sem["s" + q], count[q])
    for s in ("dfr", "drec", "dup0", "dup1", "dup2", "dup3", "dup4", "dup5", "dy"):
        g.wait_ge(T.sem[s], 16)
    g.wait_ge(T.sem.snt, 2 * D * RO)
